import numpy as np
import ml_dtypes


def mxq(x, axis, fmt="e4m3"):
    dtype, down = {"e4m3": (ml_dtypes.float8_e4m3fn, 7), "e5m2": (ml_dtypes.float8_e5m2, 14)}[fmt]
    v = np.moveaxis(np.asarray(x, np.float32).astype(ml_dtypes.bfloat16).astype(np.float64), axis, -1)
    blocks = v.reshape(v.shape[:-1] + (-1, 32))
    amax = np.abs(blocks).max(-1, keepdims=True)
    byte = np.maximum(np.where(amax > 0, np.frexp(amax)[1] - 1 + 127, 0) - down, 1)
    scale = np.exp2(byte - 127.0)
    codes = (blocks / scale).astype(np.float32).astype(dtype).astype(np.float64)
    return np.moveaxis((codes * scale).reshape(v.shape), -1, axis)


WIDE = False


def mx_kscale(k):
    if not WIDE:
        return np.ones(k)
    levels = np.array([10, -10, 5, -5, 0])
    if k % 512:
        return np.exp2(np.random.permutation(np.resize(levels, k // 32))).repeat(32)
    a = np.empty((k // 512, 16))
    for p in range(k // 512):
        a[p, :8] = np.random.permutation(np.resize(levels, 8))
        for g in range(8):
            far = levels[np.abs(levels - a[p, g]) >= 10]
            a[p, g + 8] = far[np.random.randint(len(far))]
    return np.exp2(a.ravel()).repeat(32)


def f64(x):
    return np.asarray(x).astype(np.float64)


def striped(idx):
    return np.tile(np.asarray(idx).reshape(-1, 16).T, (8, 1)).astype(np.uint16)


def unstriped(offs):
    return offs[:16].T.reshape(-1).astype(np.int64)


E2M1 = np.array([0.0, 0.5, 1.0, 1.5, 2.0, 3.0, 4.0, 6.0, -0.0, -0.5, -1.0, -1.5, -2.0, -3.0, -4.0, -6.0])


def pack_weight(w, fmt):
    k, n = w.shape
    w = f64(np.asarray(w, np.float32).astype(ml_dtypes.bfloat16)).reshape(k // 32, 32, n)
    amax = np.abs(w).max(1)
    if fmt == "e4m3":
        byte = np.frexp(amax)[1] - 1 + 127 - 7
    else:
        mant, ex = np.frexp(amax / 6.0)
        byte = np.where(mant > 0.5, ex, ex - 1) + 127
    byte = np.clip(np.where(amax > 0, byte, 1), 1, 254)
    scaled = (w * np.exp2(127.0 - byte)[:, None, :]).reshape(k, n).astype(np.float32)
    by_word = np.ascontiguousarray(scaled.reshape(k // 512, 128, 4, n).transpose(0, 1, 3, 2))
    if fmt == "e4m3":
        words = by_word.astype(ml_dtypes.float8_e4m3fn).view(np.uint8)
    else:
        c = by_word.astype(ml_dtypes.float4_e2m1fn).view(np.uint8) & 0xF
        words = (c[..., 0::2] | (c[..., 1::2] << 4)).reshape(k // 512, 128, 2 * n)
    return np.ascontiguousarray(words), np.ascontiguousarray(byte.astype(np.uint8).reshape(k // 512, 16, n))


def unpack_weight(words, scales, fmt):
    g, _, n = scales.shape
    words = np.ascontiguousarray(words).reshape(g, 128, n, -1)
    if fmt == "e4m3":
        vals = words.view(ml_dtypes.float8_e4m3fn).astype(np.float64)
    else:
        nib = np.empty((g, 128, n, 4), np.uint8)
        nib[..., 0::2] = words & 0xF
        nib[..., 1::2] = words >> 4
        vals = E2M1[nib]
    vals = vals * np.repeat(np.exp2(scales.astype(np.float64) - 127.0), 8, axis=1)[..., None]
    return vals.transpose(0, 1, 3, 2).reshape(g * 512, n)


D, T, U, I, J, G = 512, 1024, 1024, 256, 512, 64


def setup_inputs():
    n = np.random.standard_normal
    idx = np.random.permutation(T)[:I]
    idx2 = np.random.permutation(U)[:J]
    fd = mx_kscale(D)
    tabbp = pack_weight(n((D, U)) / fd[:, None], "e2m1")
    return {
        "taba": (n((D, T)) * 1 / np.sqrt(D) * fd[:, None]).astype(np.float32),
        "dtab": (n((D, T)) * 1.3 / np.sqrt(D) * fd[:, None]).astype(np.float32),
        "tabb_words": tabbp[0],
        "tabb_scales": tabbp[1],
        "targ": (n((I, J)) * 1.0).astype(np.float32),
        "base": (0.3 * n((I, J))).astype(np.float32),
        "offs": striped(idx),
        "offs2": striped(idx2),
    }


def reference(taba, dtab, tabb_words, tabb_scales, targ, base, offs, offs2):
    idx = unstriped(offs)
    idx2 = unstriped(offs2)
    tabbu = unpack_weight(tabb_words, tabb_scales, "e2m1")
    tabaidxq = mxq(f64(taba)[:, idx], 0, "e4m3")
    tabbidx2g = tabbu[:, idx2]
    s = tabaidxq.T @ tabbidx2g
    dtabidxq = mxq(f64(dtab)[:, idx], 0, "e4m3")
    ts = dtabidxq.T @ tabbidx2g
    p = np.exp(s)
    s1g = p.reshape(I, G, J // G).sum(axis=2)
    r1g = np.sqrt(s1g)
    z = np.sum(r1g, axis=1, keepdims=True)
    k1 = r1g / s1g / z
    kr = np.repeat(k1, J // G, axis=1)
    dkr = f64(targ) / (p * kr * 512.0 + 1.0) * 512.0 * p
    dk1 = dkr.reshape(I, G, J // G).sum(axis=2)
    dz = np.sum(dk1 * r1g / s1g / np.square(z) * (-1.0), axis=1, keepdims=True)
    dr1g = dk1 / z / s1g + dz
    ds1g = dr1g * 0.5 / np.sqrt(s1g) - dk1 / z * r1g / np.square(s1g)
    r1 = np.repeat(ds1g, J // G, axis=1)
    dp = f64(targ) / (p * kr * 512.0 + 1.0) * 512.0 * kr + r1
    xp = ts * p
    xs1g = xp.reshape(I, G, J // G).sum(axis=2)
    xr1g = xs1g * 0.5 / r1g
    xz = np.sum(xr1g, axis=1, keepdims=True)
    xk1 = ((xr1g - xs1g * r1g / s1g) / s1g - xz * r1g / s1g / z) / z
    xkr = np.repeat(xk1, J // G, axis=1)
    xdkr = (xp * kr + xkr * p) * 512.0 * f64(targ) / np.square(p * kr * 512.0 + 1.0) * (-1.0) * 512.0 * p + xp * f64(targ) / (p * kr * 512.0 + 1.0) * 512.0
    xdk1 = xdkr.reshape(I, G, J // G).sum(axis=2)
    xdz = np.sum((xdk1 * r1g / s1g + (xr1g - xs1g * r1g / s1g) / s1g * dk1 - xz * z * 2.0 * dk1 * r1g / s1g / np.square(z)) / np.square(z) * (-1.0), axis=1, keepdims=True)
    xdr1g = ((xdk1 - xz * dk1 / z) / z - xs1g * dk1 / z / s1g) / s1g + xdz
    xds1g = (xdr1g * 0.5 - xs1g * 0.5 / np.sqrt(s1g) * dr1g * 0.5 / np.sqrt(s1g)) / np.sqrt(s1g) - ((xdk1 - xz * dk1 / z) / z * r1g + xr1g * dk1 / z - xs1g * s1g * 2.0 * dk1 / z * r1g / np.square(s1g)) / np.square(s1g)
    xr1 = np.repeat(xds1g, J // G, axis=1)
    xdp = (xp * kr + xkr * p) * 512.0 * f64(targ) / np.square(p * kr * 512.0 + 1.0) * (-1.0) * 512.0 * kr + xkr * f64(targ) / (p * kr * 512.0 + 1.0) * 512.0 + xr1
    xds = xdp * p + xp * dp
    y = xds + f64(base)
    return y

@@ -1,0 +1,198 @@
+from contextlib import ExitStack
+
+import concourse.mybir as mybir
+from concourse.masks import make_identity
+
+D, T, U, I, J, G = 512, 1024, 1024, 256, 512, 64
+E = J // G
+P = 128
+PACK = 4
+HALVES = I // P
+FLOPS = 2 * 2 * D * I * J
+
+F32 = mybir.dt.float32
+BF16 = mybir.dt.bfloat16
+I32 = mybir.dt.int32
+U32 = mybir.dt.uint32
+U16 = mybir.dt.uint16
+U8 = mybir.dt.uint8
+FP8X4 = mybir.dt.float8_e4m3fn_x4
+FP4X4 = mybir.dt.float4_e2m1fn_x4
+ACT = mybir.ActivationFunctionType
+ALU = mybir.AluOpType
+AX = mybir.AxisListType
+
+
+def tile_attend_hvblockshares_kernel(tc, taba, dtab, tabb_words, tabb_scales, targ, base, offs, offs2, out):
+    nc = tc.nc
+    with ExitStack() as ctx:
+        lists = ctx.enter_context(tc.tile_pool(name="lists", bufs=1))
+        keep = ctx.enter_context(tc.tile_pool(name="keep", bufs=1))
+        psum = ctx.enter_context(tc.psum_pool(name="psum", bufs=1))
+
+        def sb(name, shape, dtype=F32):
+            return keep.tile(shape, dtype, name=name, align_bytes=64)
+
+        def grouped(ap):
+            return ap.rearrange("p (g e) -> p g e", e=E)
+
+        def spread(ap):
+            return ap.unsqueeze(2).to_broadcast([P, G, E])
+
+        rows_list = lists.tile([P, I // 16], U16, name="rows_list")
+        cols_list = lists.tile([P, J // 16], U16, name="cols_list")
+        words = sb("words", [P, U], U16)
+        scales = sb("scales", [P, U], U8)
+        a_planes = [sb(f"a_plane{t}", [P, T]) for t in range(PACK)]
+        d_planes = [sb(f"d_plane{t}", [P, T]) for t in range(PACK)]
+        targ_sb = [sb(f"targ{h}", [P, J]) for h in range(HALVES)]
+        base_sb = [sb(f"base{h}", [P, J]) for h in range(HALVES)]
+
+        nc.gpsimd.memset(scales[:].bitcast(I32), 0)
+        ident = sb("ident", [P, P])
+        make_identity(nc, ident[:])
+        a_rows = taba.rearrange("(p t) n -> p t n", t=PACK)
+        d_rows = dtab.rearrange("(p t) n -> p t n", t=PACK)
+        nc.sync.dma_start(rows_list[:], offs)
+        nc.sync.dma_start(cols_list[:], offs2)
+        for t in range(2):
+            nc.sync.dma_start(a_planes[t][:], a_rows[:, t, :])
+        for q in range(4):
+            nc.sync.dma_start(scales[32 * q : 32 * q + 4, :].bitcast(I32), tabb_scales[0, 4 * q : 4 * q + 4, :].bitcast(I32))
+        nc.sync.dma_start(words[:].bitcast(I32), tabb_words[0].bitcast(I32))
+        for t in range(2, PACK):
+            nc.sync.dma_start(a_planes[t][:], a_rows[:, t, :])
+        for t in range(PACK):
+            nc.sync.dma_start(d_planes[t][:], d_rows[:, t, :])
+        for h in range(HALVES):
+            nc.sync.dma_start(targ_sb[h][:], targ[h * P : (h + 1) * P, :])
+        for h in range(HALVES):
+            nc.sync.dma_start(base_sb[h][:], base[h * P : (h + 1) * P, :])
+
+        b_words = sb("b_words", [P, J], U16)
+        b_scales = sb("b_scales", [P, J], U8)
+        nc.vector.tensor_copy(b_scales[:], scales[:].indirect(cols_list[:]))
+        nc.vector.tensor_copy(b_words[:], words[:].indirect(cols_list[:]))
+
+        a_picked = sb("a_picked", [P, 2, I], BF16)
+        a_woven = [sb(f"a_woven{h}", [P, P, PACK], BF16) for h in range(HALVES)]
+        for t in range(2):
+            nc.scalar.activation(a_picked[:, t, :], a_planes[t][:].indirect(rows_list[:]), ACT.Copy)
+        for h in range(HALVES):
+            nc.scalar.copy(a_woven[h][:, :, 0:2], a_picked[:, :, h * P : (h + 1) * P].rearrange("p t n -> p n t"))
+        for t in range(2, PACK):
+            for h in range(HALVES):
+                nc.vector.tensor_copy(a_woven[h][:, :, t], a_planes[t][:].indirect(rows_list[:, 8 * h : 8 * h + 8]))
+        s_ps = [psum.tile([P, J], F32, name=f"s_ps{h}", tag=f"row_bank{h}") for h in range(HALVES)]
+        t_ps = [psum.tile([P, J], F32, name=f"t_ps{h}") for h in range(HALVES)]
+        p = [sb(f"p{h}", [P, J]) for h in range(HALVES)]
+        s1g = sb("s1g", [P, HALVES, G])
+        for h in range(HALVES):
+            codes = sb(f"a_codes{h}", [P, P], U32)
+            plane = sb(f"a_scales{h}", [P, P], U8)
+            nc.vector.quantize_mx(out=codes[:].bitcast(FP8X4), scales=plane[:], in_=a_woven[h][:].rearrange("p n t -> p (n t)"))
+            nc.tensor.matmul_mx(out=s_ps[h][:], lhsT=codes[:].bitcast(FP8X4), lhsT_scale=plane[:],
+                                rhs=b_words[:].bitcast(FP4X4), rhs_scale=b_scales[:], start=True, stop=True)
+            nc.scalar.activation(p[h][:], s_ps[h][:], ACT.Exp)
+        for h in range(HALVES):
+            nc.vector.tensor_reduce(s1g[:, h, :], grouped(p[h][:]), AX.X, ALU.add)
+
+        rs = sb("rs", [P, HALVES, G])
+        nc.scalar.activation(rs[:], s1g[:], ACT.Abs_reciprocal_sqrt)
+
+        d_picked = sb("d_picked", [P, PACK, I], BF16)
+        for t in range(PACK):
+            if t > 0:
+                nc.vector.tensor_copy(d_picked[:, t, :], d_planes[t][:].indirect(rows_list[:]))
+            else:
+                nc.scalar.activation(d_picked[:, t, :], d_planes[t][:].indirect(rows_list[:]), ACT.Copy)
+
+        root = sb("root", [P, HALVES, G])
+        z = sb("z", [P, HALVES])
+        iz = sb("iz", [P, HALVES])
+        piz = sb("piz", [P, HALVES])
+        hpiz = sb("hpiz", [P, HALVES])
+        n = [sb(f"n{h}", [P, J]) for h in range(HALVES)]
+        dh = [sb(f"dh{h}", [P, J]) for h in range(HALVES)]
+        d = [sb(f"d{h}", [P, J]) for h in range(HALVES)]
+        for h in range(HALVES):
+            nc.vector.scalar_tensor_tensor(root[:, h, :], s1g[:, h, :], 1.0 / 512.0, rs[:, h, :], ALU.mult, ALU.mult, accum_out=z[:, h : h + 1])
+        nc.vector.tensor_tensor(grouped(n[0][:]), grouped(p[0][:]), spread(rs[:, 0, :]), ALU.mult)
+        nc.vector.reciprocal(iz[:], z[:])
+        nc.vector.tensor_tensor(grouped(n[1][:]), grouped(p[1][:]), spread(rs[:, 1, :]), ALU.mult)
+        for h in range(HALVES):
+            nc.scalar.activation(dh[h][:], n[h][:], ACT.Abs_reciprocal_sqrt, bias=1.0, scale=iz[:, h : h + 1])
+            nc.scalar.activation(d[h][:], dh[h][:], ACT.Square)
+        nc.scalar.activation(piz[:], iz[:], ACT.Copy, scale=1.0 / 512.0)
+        nc.scalar.activation(hpiz[:], iz[:], ACT.Copy, scale=1.0 / 1024.0)
+
+        d_woven = sb("d_woven", [P, I, PACK], BF16)
+        nc.vector.tensor_copy(d_woven[:], d_picked[:].rearrange("p t n -> p n t"))
+        d_codes = sb("d_codes", [P, I], U32)
+        d_scales = sb("d_scales", [P, I], U8)
+        nc.vector.quantize_mx(out=d_codes[:].bitcast(FP8X4), scales=d_scales[:], in_=d_woven[:].rearrange("p n t -> p (n t)"))
+        for h in range(HALVES):
+            nc.tensor.matmul_mx(out=t_ps[h][:], lhsT=d_codes[:, h * P : (h + 1) * P].bitcast(FP8X4), lhsT_scale=d_scales[:, h * P : (h + 1) * P],
+                                rhs=b_words[:].bitcast(FP4X4), rhs_scale=b_scales[:], start=True, stop=True)
+
+        big = {}
+        small = {}
+        one = {}
+        for h in range(HALVES):
+            for name in ("x", "nv", "tau", "dw", "ax", "dn", "y", "sum_t"):
+                big[name, h] = sb(f"{name}{h}", [P, J])
+            for name in ("xg", "hm", "a2", "e1", "dwg", "d1", "dd"):
+                small[name, h] = sb(f"{name}{h}", [P, G])
+            for name in ("xt", "m2", "nwt", "b1", "b1x2", "nb", "dwt", "c2"):
+                one[name, h] = sb(f"{name}{h}", [P, 1])
+        nw = sb("nw", [P, HALVES * J])
+        acc = [psum.tile([P, J], F32, name=f"acc{h}") for h in range(HALVES)]
+        nwg_t_ps = psum.tile([P, P], F32, name="nwg_t_ps")
+        nwg_ps = psum.tile([P, P], F32, name="nwg_ps")
+        nwg_t = sb("nwg_t", [P, P])
+
+        def add_turned(h, src, first, last):
+            for b in range(J // P):
+                cols = slice(b * P, (b + 1) * P)
+                nc.tensor.matmul(acc[h][:, cols], src[:, cols], ident[:], start=(first and b == 0), stop=(last and b == J // P - 1), is_transpose=True)
+
+        v = nc.vector
+        for h in range(HALVES):
+            nw_h = nw[:, h * J : (h + 1) * J]
+            v.scalar_tensor_tensor(nw_h, d[h][:], 1.0, targ_sb[h][:], ALU.subtract, ALU.mult, accum_out=one["nwt", h][:])
+            v.scalar_tensor_tensor(big["x", h][:], t_ps[h][:], 0.5, n[h][:], ALU.mult, ALU.mult, accum_out=one["xt", h][:])
+            v.tensor_tensor(big["nv", h][:], nw_h, d[h][:], ALU.mult)
+            v.tensor_reduce(small["xg", h][:], grouped(big["x", h][:]), AX.X, ALU.add)
+            v.tensor_tensor(small["hm", h][:], small["xg", h][:], rs[:, h, :], ALU.mult)
+            nc.scalar.activation(one["m2", h][:], one["xt", h][:], ACT.Copy, scale=piz[:, h : h + 1])
+            nc.scalar.activation(one["b1x2", h][:], one["nwt", h][:], ACT.Copy, scale=piz[:, h : h + 1])
+            nc.scalar.activation(one["b1", h][:], one["nwt", h][:], ACT.Copy, scale=hpiz[:, h : h + 1])
+            nc.scalar.activation(one["nb", h][:], one["b1", h][:], ACT.Copy, scale=one["m2", h][:])
+        for e in range(E):
+            nc.tensor.matmul(nwg_t_ps[:], nw[:, e : HALVES * J : E], ident[:], start=(e == 0), stop=(e == E - 1), is_transpose=True)
+        nc.scalar.copy(nwg_t[:], nwg_t_ps[:])
+        nc.tensor.transpose(nwg_ps[:], nwg_t[:], ident[:])
+        for h in range(HALVES):
+            add_turned(h, base_sb[h], True, False)
+        for h in range(HALVES):
+            v.scalar_tensor_tensor(grouped(big["tau", h][:]), grouped(t_ps[h][:]), one["m2", h][:], spread(small["hm", h][:]), ALU.subtract, ALU.subtract)
+            v.scalar_tensor_tensor(big["dw", h][:], big["nv", h][:], -1.0, big["tau", h][:], ALU.mult, ALU.mult, accum_out=one["dwt", h][:])
+            add_turned(h, big["dw", h], False, False)
+        for h in range(HALVES):
+            v.tensor_reduce(small["dwg", h][:], grouped(big["dw", h][:]), AX.X, ALU.add)
+            v.tensor_tensor(small["a2", h][:], nwg_ps[:, h * G : (h + 1) * G], rs[:, h, :], ALU.mult)
+            nc.scalar.activation(one["c2", h][:], one["dwt", h][:], ACT.Identity, bias=one["nb", h][:], scale=hpiz[:, h : h + 1])
+            v.scalar_tensor_tensor(small["d1", h][:], small["dwg", h][:], -0.5, rs[:, h, :], ALU.mult, ALU.mult)
+            v.scalar_tensor_tensor(grouped(big["ax", h][:]), spread(small["a2", h][:]), one["b1x2", h][:], grouped(big["x", h][:]), ALU.add, ALU.mult)
+            add_turned(h, big["ax", h], False, True)
+            nc.scalar.copy(big["sum_t", h][:], acc[h][:])
+            v.scalar_tensor_tensor(small["e1", h][:], small["a2", h][:], one["b1", h][:], small["hm", h][:], ALU.add, ALU.mult)
+        for h in range(HALVES):
+            back = psum.tile([P, J], F32, name=f"back{h}", tag=f"row_bank{h}")
+            for b in range(J // P):
+                cols = slice(b * P, (b + 1) * P)
+                nc.tensor.transpose(back[:, cols], big["sum_t", h][:, cols], ident[:])
+            v.tensor_tensor(small["dd", h][:], small["d1", h][:], small["e1", h][:], ALU.subtract)
+            v.scalar_tensor_tensor(grouped(big["dn", h][:]), spread(small["dd", h][:]), one["c2", h][:], grouped(n[h][:]), ALU.subtract, ALU.mult)
+            v.tensor_tensor(big["y", h][:], back[:], big["dn", h][:], ALU.add)
+            nc.sync.dma_start(out[h * P : (h + 1) * P, :], big["y", h][:])

@@ -53,13 +53,13 @@ def tile_attend_hvblockshares_kernel(tc, taba, dtab, tabb_words, tabb_scales, ta
         make_identity(nc, ident[:])
         a_rows = taba.rearrange("(p t) n -> p t n", t=PACK)
         d_rows = dtab.rearrange("(p t) n -> p t n", t=PACK)
-        nc.sync.dma_start(rows_list[:], offs)
         nc.sync.dma_start(cols_list[:], offs2)
+        nc.sync.dma_start(words[:].bitcast(I32), tabb_words[0].bitcast(I32))
+        nc.sync.dma_start(rows_list[:], offs)
         for t in range(2):
             nc.sync.dma_start(a_planes[t][:], a_rows[:, t, :])
         for q in range(4):
             nc.sync.dma_start(scales[32 * q : 32 * q + 4, :].bitcast(I32), tabb_scales[0, 4 * q : 4 * q + 4, :].bitcast(I32))
-        nc.sync.dma_start(words[:].bitcast(I32), tabb_words[0].bitcast(I32))
         for t in range(2, PACK):
             nc.sync.dma_start(a_planes[t][:], a_rows[:, t, :])
         for t in range(PACK):
@@ -71,8 +71,8 @@ def tile_attend_hvblockshares_kernel(tc, taba, dtab, tabb_words, tabb_scales, ta
 
         b_words = sb("b_words", [P, J], U16)
         b_scales = sb("b_scales", [P, J], U8)
-        nc.vector.tensor_copy(b_scales[:], scales[:].indirect(cols_list[:]))
         nc.vector.tensor_copy(b_words[:], words[:].indirect(cols_list[:]))
+        nc.vector.tensor_copy(b_scales[:], scales[:].indirect(cols_list[:]))
 
         a_picked = sb("a_picked", [P, 2, I], BF16)
         a_woven = [sb(f"a_woven{h}", [P, P, PACK], BF16) for h in range(HALVES)]
@@ -83,7 +83,6 @@ def tile_attend_hvblockshares_kernel(tc, taba, dtab, tabb_words, tabb_scales, ta
         for t in range(2, PACK):
             for h in range(HALVES):
                 nc.vector.tensor_copy(a_woven[h][:, :, t], a_planes[t][:].indirect(rows_list[:, 8 * h : 8 * h + 8]))
-        s_ps = [psum.tile([P, J], F32, name=f"s_ps{h}", tag=f"row_bank{h}") for h in range(HALVES)]
         t_ps = [psum.tile([P, J], F32, name=f"t_ps{h}") for h in range(HALVES)]
         p = [sb(f"p{h}", [P, J]) for h in range(HALVES)]
         s1g = sb("s1g", [P, HALVES, G])
@@ -91,21 +90,22 @@ def tile_attend_hvblockshares_kernel(tc, taba, dtab, tabb_words, tabb_scales, ta
             codes = sb(f"a_codes{h}", [P, P], U32)
             plane = sb(f"a_scales{h}", [P, P], U8)
             nc.vector.quantize_mx(out=codes[:].bitcast(FP8X4), scales=plane[:], in_=a_woven[h][:].rearrange("p n t -> p (n t)"))
-            nc.tensor.matmul_mx(out=s_ps[h][:], lhsT=codes[:].bitcast(FP8X4), lhsT_scale=plane[:],
-                                rhs=b_words[:].bitcast(FP4X4), rhs_scale=b_scales[:], start=True, stop=True)
-            nc.scalar.activation(p[h][:], s_ps[h][:], ACT.Exp)
+            for k in range(2):
+                cols = slice(k * J // 2, (k + 1) * J // 2)
+                s_ps = psum.tile([P, J // 2], F32, name=f"s_ps{h}{k}", tag=f"bank{h}{k}")
+                nc.tensor.matmul_mx(out=s_ps[:], lhsT=codes[:].bitcast(FP8X4), lhsT_scale=plane[:],
+                                    rhs=b_words[:, cols].bitcast(FP4X4), rhs_scale=b_scales[:, cols], start=True, stop=True)
+                nc.scalar.activation(p[h][:, cols], s_ps[:], ACT.Exp)
         for h in range(HALVES):
             nc.vector.tensor_reduce(s1g[:, h, :], grouped(p[h][:]), AX.X, ALU.add)
 
         rs = sb("rs", [P, HALVES, G])
         nc.scalar.activation(rs[:], s1g[:], ACT.Abs_reciprocal_sqrt)
 
-        d_picked = sb("d_picked", [P, PACK, I], BF16)
-        for t in range(PACK):
-            if t > 0:
-                nc.vector.tensor_copy(d_picked[:, t, :], d_planes[t][:].indirect(rows_list[:]))
-            else:
-                nc.scalar.activation(d_picked[:, t, :], d_planes[t][:].indirect(rows_list[:]), ACT.Copy)
+        d_picked = keep.tile([P, PACK, I], BF16, name="d_picked", tag="a_woven1", align_bytes=64)
+        for t in range(PACK - 1):
+            nc.vector.tensor_copy(d_picked[:, t, :], d_planes[t][:].indirect(rows_list[:]))
+        nc.scalar.activation(d_picked[:, PACK - 1, :], d_planes[PACK - 1][:].indirect(rows_list[:]), ACT.Copy)
 
         root = sb("root", [P, HALVES, G])
         z = sb("z", [P, HALVES])
@@ -119,15 +119,19 @@ def tile_attend_hvblockshares_kernel(tc, taba, dtab, tabb_words, tabb_scales, ta
             nc.vector.scalar_tensor_tensor(root[:, h, :], s1g[:, h, :], 1.0 / 512.0, rs[:, h, :], ALU.mult, ALU.mult, accum_out=z[:, h : h + 1])
         nc.vector.tensor_tensor(grouped(n[0][:]), grouped(p[0][:]), spread(rs[:, 0, :]), ALU.mult)
         nc.vector.reciprocal(iz[:], z[:])
+        d_woven = keep.tile([P, I, PACK], BF16, name="d_woven", tag="z", align_bytes=64)
+        nc.vector.tensor_copy(d_woven[:], d_picked[:].rearrange("p t n -> p n t"))
         nc.vector.tensor_tensor(grouped(n[1][:]), grouped(p[1][:]), spread(rs[:, 1, :]), ALU.mult)
         for h in range(HALVES):
-            nc.scalar.activation(dh[h][:], n[h][:], ACT.Abs_reciprocal_sqrt, bias=1.0, scale=iz[:, h : h + 1])
-            nc.scalar.activation(d[h][:], dh[h][:], ACT.Square)
+            for k in range(2):
+                cols = slice(k * J // 2, (k + 1) * J // 2)
+                nc.scalar.activation(dh[h][:, cols], n[h][:, cols], ACT.Abs_reciprocal_sqrt, bias=1.0, scale=iz[:, h : h + 1])
+            for k in range(2):
+                cols = slice(k * J // 2, (k + 1) * J // 2)
+                nc.scalar.activation(d[h][:, cols], dh[h][:, cols], ACT.Square)
         nc.scalar.activation(piz[:], iz[:], ACT.Copy, scale=1.0 / 512.0)
         nc.scalar.activation(hpiz[:], iz[:], ACT.Copy, scale=1.0 / 1024.0)
 
-        d_woven = sb("d_woven", [P, I, PACK], BF16)
-        nc.vector.tensor_copy(d_woven[:], d_picked[:].rearrange("p t n -> p n t"))
         d_codes = sb("d_codes", [P, I], U32)
         d_scales = sb("d_scales", [P, I], U8)
         nc.vector.quantize_mx(out=d_codes[:].bitcast(FP8X4), scales=d_scales[:], in_=d_woven[:].rearrange("p n t -> p (n t)"))
@@ -139,14 +143,14 @@ def tile_attend_hvblockshares_kernel(tc, taba, dtab, tabb_words, tabb_scales, ta
         small = {}
         one = {}
         for h in range(HALVES):
-            for name in ("x", "nv", "tau", "dw", "ax", "dn", "y", "sum_t"):
+            for name in ("x", "tau", "dw", "ax", "dn", "y", "sum_t"):
                 big[name, h] = sb(f"{name}{h}", [P, J])
-            for name in ("xg", "hm", "a2", "e1", "dwg", "d1", "dd"):
+            for name in ("xg", "hm", "e1", "dwg", "d1", "dd"):
                 small[name, h] = sb(f"{name}{h}", [P, G])
             for name in ("xt", "m2", "nwt", "b1", "b1x2", "nb", "dwt", "c2"):
                 one[name, h] = sb(f"{name}{h}", [P, 1])
         nw = sb("nw", [P, HALVES * J])
-        acc = [psum.tile([P, J], F32, name=f"acc{h}") for h in range(HALVES)]
+        acc = [psum.tile([P, J], F32, name=f"acc{h}", tag=f"bank{h}1") for h in range(HALVES)]
         nwg_t_ps = psum.tile([P, P], F32, name="nwg_t_ps")
         nwg_ps = psum.tile([P, P], F32, name="nwg_ps")
         nwg_t = sb("nwg_t", [P, P])
@@ -156,43 +160,69 @@ def tile_attend_hvblockshares_kernel(tc, taba, dtab, tabb_words, tabb_scales, ta
                 cols = slice(b * P, (b + 1) * P)
                 nc.tensor.matmul(acc[h][:, cols], src[:, cols], ident[:], start=(first and b == 0), stop=(last and b == J // P - 1), is_transpose=True)
 
+        def turn_back(h):
+            nc.scalar.copy(big["sum_t", h][:], acc[h][:])
+            back = psum.tile([P, J], F32, name=f"back{h}", tag=f"bank{h}0")
+            for b in range(J // P):
+                cols = slice(b * P, (b + 1) * P)
+                nc.tensor.transpose(back[:, cols], big["sum_t", h][:, cols], ident[:])
+            return back
+
         v = nc.vector
         for h in range(HALVES):
-            nw_h = nw[:, h * J : (h + 1) * J]
-            v.scalar_tensor_tensor(nw_h, d[h][:], 1.0, targ_sb[h][:], ALU.subtract, ALU.mult, accum_out=one["nwt", h][:])
+            v.scalar_tensor_tensor(nw[:, h * J : (h + 1) * J], d[h][:], 1.0, targ_sb[h][:], ALU.subtract, ALU.mult, accum_out=one["nwt", h][:])
             v.scalar_tensor_tensor(big["x", h][:], t_ps[h][:], 0.5, n[h][:], ALU.mult, ALU.mult, accum_out=one["xt", h][:])
-            v.tensor_tensor(big["nv", h][:], nw_h, d[h][:], ALU.mult)
-            v.tensor_reduce(small["xg", h][:], grouped(big["x", h][:]), AX.X, ALU.add)
-            v.tensor_tensor(small["hm", h][:], small["xg", h][:], rs[:, h, :], ALU.mult)
+        for e in range(E):
+            nc.tensor.matmul(nwg_t_ps[:], nw[:, e : HALVES * J : E], ident[:], start=(e == 0), stop=(e == E - 1), is_transpose=True)
+        for h in range(HALVES):
+            add_turned(h, base_sb[h], True, False)
+        nv = [keep.tile([P, J], F32, name=f"nv{h}", tag=f"targ{HALVES - 1 - h}", align_bytes=64) for h in range(HALVES)]
+        for h in range(HALVES):
+            nc.gpsimd.tensor_tensor(nv[h][:], nw[:, h * J : (h + 1) * J], d[h][:], ALU.mult)
+        for h in range(HALVES):
             nc.scalar.activation(one["m2", h][:], one["xt", h][:], ACT.Copy, scale=piz[:, h : h + 1])
             nc.scalar.activation(one["b1x2", h][:], one["nwt", h][:], ACT.Copy, scale=piz[:, h : h + 1])
             nc.scalar.activation(one["b1", h][:], one["nwt", h][:], ACT.Copy, scale=hpiz[:, h : h + 1])
             nc.scalar.activation(one["nb", h][:], one["b1", h][:], ACT.Copy, scale=one["m2", h][:])
-        for e in range(E):
-            nc.tensor.matmul(nwg_t_ps[:], nw[:, e : HALVES * J : E], ident[:], start=(e == 0), stop=(e == E - 1), is_transpose=True)
         nc.scalar.copy(nwg_t[:], nwg_t_ps[:])
         nc.tensor.transpose(nwg_ps[:], nwg_t[:], ident[:])
         for h in range(HALVES):
-            add_turned(h, base_sb[h], True, False)
-        for h in range(HALVES):
+            v.tensor_reduce(small["xg", h][:], grouped(big["x", h][:]), AX.X, ALU.add)
+            v.tensor_tensor(small["hm", h][:], small["xg", h][:], rs[:, h, :], ALU.mult)
+
+        def tau(h):
             v.scalar_tensor_tensor(grouped(big["tau", h][:]), grouped(t_ps[h][:]), one["m2", h][:], spread(small["hm", h][:]), ALU.subtract, ALU.subtract)
-            v.scalar_tensor_tensor(big["dw", h][:], big["nv", h][:], -1.0, big["tau", h][:], ALU.mult, ALU.mult, accum_out=one["dwt", h][:])
+
+        def dw(h):
+            v.scalar_tensor_tensor(big["dw", h][:], nv[h][:], -1.0, big["tau", h][:], ALU.mult, ALU.mult, accum_out=one["dwt", h][:])
+            nc.scalar.activation(one["c2", h][:], one["dwt", h][:], ACT.Identity, bias=one["nb", h][:], scale=hpiz[:, h : h + 1])
             add_turned(h, big["dw", h], False, False)
+
+        def ax(h):
+            v.scalar_tensor_tensor(grouped(big["ax", h][:]), spread(a2[:, h, :]), one["b1x2", h][:], grouped(big["x", h][:]), ALU.add, ALU.mult)
+            add_turned(h, big["ax", h], False, True)
+            return turn_back(h)
+
+        tau(0)
+        dw(0)
+        tau(1)
+        a2 = keep.tile([P, HALVES, G], F32, name="a2", tag="m21", align_bytes=64)
+        v.tensor_tensor(a2[:], nwg_ps[:].rearrange("p (h g) -> p h g", h=HALVES), rs[:], ALU.mult)
+        back = [ax(0)]
+        dw(1)
+        back.append(ax(1))
         for h in range(HALVES):
             v.tensor_reduce(small["dwg", h][:], grouped(big["dw", h][:]), AX.X, ALU.add)
-            v.tensor_tensor(small["a2", h][:], nwg_ps[:, h * G : (h + 1) * G], rs[:, h, :], ALU.mult)
-            nc.scalar.activation(one["c2", h][:], one["dwt", h][:], ACT.Identity, bias=one["nb", h][:], scale=hpiz[:, h : h + 1])
-            v.scalar_tensor_tensor(small["d1", h][:], small["dwg", h][:], -0.5, rs[:, h, :], ALU.mult, ALU.mult)
-            v.scalar_tensor_tensor(grouped(big["ax", h][:]), spread(small["a2", h][:]), one["b1x2", h][:], grouped(big["x", h][:]), ALU.add, ALU.mult)
-            add_turned(h, big["ax", h], False, True)
-            nc.scalar.copy(big["sum_t", h][:], acc[h][:])
-            v.scalar_tensor_tensor(small["e1", h][:], small["a2", h][:], one["b1", h][:], small["hm", h][:], ALU.add, ALU.mult)
+            v.scalar_tensor_tensor(small["e1", h][:], a2[:, h, :], one["b1", h][:], small["hm", h][:], ALU.add, ALU.mult)
         for h in range(HALVES):
-            back = psum.tile([P, J], F32, name=f"back{h}", tag=f"row_bank{h}")
-            for b in range(J // P):
-                cols = slice(b * P, (b + 1) * P)
-                nc.tensor.transpose(back[:, cols], big["sum_t", h][:, cols], ident[:])
+            v.scalar_tensor_tensor(small["d1", h][:], small["dwg", h][:], -0.5, rs[:, h, :], ALU.mult, ALU.mult)
+        for h in range(HALVES):
             v.tensor_tensor(small["dd", h][:], small["d1", h][:], small["e1", h][:], ALU.subtract)
+        for h in range(HALVES):
             v.scalar_tensor_tensor(grouped(big["dn", h][:]), spread(small["dd", h][:]), one["c2", h][:], grouped(n[h][:]), ALU.subtract, ALU.mult)
-            v.tensor_tensor(big["y", h][:], back[:], big["dn", h][:], ALU.add)
-            nc.sync.dma_start(out[h * P : (h + 1) * P, :], big["y", h][:])
+        for h in range(HALVES):
+            pieces = 1 + h
+            for k in range(pieces):
+                cols = slice(k * J // pieces, (k + 1) * J // pieces)
+                v.tensor_tensor(big["y", h][:, cols], back[h][:, cols], big["dn", h][:, cols], ALU.add)
+                nc.sync.dma_start(out[h * P : (h + 1) * P, cols], big["y", h][:, cols])

@@ -46,7 +46,6 @@ def tile_attend_hvblockshares_kernel(tc, taba, dtab, tabb_words, tabb_scales, ta
         a_planes = [sb(f"a_plane{t}", [P, T]) for t in range(PACK)]
         d_planes = [sb(f"d_plane{t}", [P, T]) for t in range(PACK)]
         targ_sb = [sb(f"targ{h}", [P, J]) for h in range(HALVES)]
-        base_sb = [sb(f"base{h}", [P, J]) for h in range(HALVES)]
 
         nc.gpsimd.memset(scales[:].bitcast(I32), 0)
         ident = sb("ident", [P, P])
@@ -66,8 +65,6 @@ def tile_attend_hvblockshares_kernel(tc, taba, dtab, tabb_words, tabb_scales, ta
             nc.sync.dma_start(d_planes[t][:], d_rows[:, t, :])
         for h in range(HALVES):
             nc.sync.dma_start(targ_sb[h][:], targ[h * P : (h + 1) * P, :])
-        for h in range(HALVES):
-            nc.sync.dma_start(base_sb[h][:], base[h * P : (h + 1) * P, :])
 
         b_words = sb("b_words", [P, J], U16)
         b_scales = sb("b_scales", [P, J], U8)
@@ -117,11 +114,29 @@ def tile_attend_hvblockshares_kernel(tc, taba, dtab, tabb_words, tabb_scales, ta
         d = [sb(f"d{h}", [P, J]) for h in range(HALVES)]
         for h in range(HALVES):
             nc.vector.scalar_tensor_tensor(root[:, h, :], s1g[:, h, :], 1.0 / 512.0, rs[:, h, :], ALU.mult, ALU.mult, accum_out=z[:, h : h + 1])
-        nc.vector.tensor_tensor(grouped(n[0][:]), grouped(p[0][:]), spread(rs[:, 0, :]), ALU.mult)
+        def half_of(ap, k):
+            return ap[:, k * J // 2 : (k + 1) * J // 2].rearrange("p (g e) -> p g e", e=E)
+
+        def n_piece(k):
+            nc.vector.tensor_tensor(half_of(n[0], k), half_of(p[0], k), rs[:, 0, k * G // 2 : (k + 1) * G // 2].unsqueeze(2).to_broadcast([P, G // 2, E]), ALU.mult)
+
+        n_piece(0)
         nc.vector.reciprocal(iz[:], z[:])
-        d_woven = keep.tile([P, I, PACK], BF16, name="d_woven", tag="z", align_bytes=64)
-        nc.vector.tensor_copy(d_woven[:], d_picked[:].rearrange("p t n -> p n t"))
+        n_piece(1)
+        d_woven = [keep.tile([P, P, PACK], BF16, name=f"d_woven{h}", tag=("z", "root")[h], align_bytes=64) for h in range(HALVES)]
+        d_codes = [sb(f"d_codes{h}", [P, P], U32) for h in range(HALVES)]
+        d_scales = [sb(f"d_scales{h}", [P, P], U8) for h in range(HALVES)]
+        for h in range(HALVES):
+            nc.vector.tensor_copy(d_woven[h][:], d_picked[:, :, h * P : (h + 1) * P].rearrange("p t n -> p n t"))
+
+        def tangent_scores(h):
+            nc.vector.quantize_mx(out=d_codes[h][:].bitcast(FP8X4), scales=d_scales[h][:], in_=d_woven[h][:].rearrange("p n t -> p (n t)"))
+            nc.tensor.matmul_mx(out=t_ps[h][:], lhsT=d_codes[h][:].bitcast(FP8X4), lhsT_scale=d_scales[h][:],
+                                rhs=b_words[:].bitcast(FP4X4), rhs_scale=b_scales[:], start=True, stop=True)
+
+        tangent_scores(0)
         nc.vector.tensor_tensor(grouped(n[1][:]), grouped(p[1][:]), spread(rs[:, 1, :]), ALU.mult)
+        tangent_scores(1)
         for h in range(HALVES):
             for k in range(2):
                 cols = slice(k * J // 2, (k + 1) * J // 2)
@@ -131,13 +146,9 @@ def tile_attend_hvblockshares_kernel(tc, taba, dtab, tabb_words, tabb_scales, ta
                 nc.scalar.activation(d[h][:, cols], dh[h][:, cols], ACT.Square)
         nc.scalar.activation(piz[:], iz[:], ACT.Copy, scale=1.0 / 512.0)
         nc.scalar.activation(hpiz[:], iz[:], ACT.Copy, scale=1.0 / 1024.0)
-
-        d_codes = sb("d_codes", [P, I], U32)
-        d_scales = sb("d_scales", [P, I], U8)
-        nc.vector.quantize_mx(out=d_codes[:].bitcast(FP8X4), scales=d_scales[:], in_=d_woven[:].rearrange("p n t -> p (n t)"))
+        base_sb = [keep.tile([P, J], F32, name=f"base{h}", tag=("d_codes1", "d_scales1")[h], align_bytes=64) for h in range(HALVES)]
         for h in range(HALVES):
-            nc.tensor.matmul_mx(out=t_ps[h][:], lhsT=d_codes[:, h * P : (h + 1) * P].bitcast(FP8X4), lhsT_scale=d_scales[:, h * P : (h + 1) * P],
-                                rhs=b_words[:].bitcast(FP4X4), rhs_scale=b_scales[:], start=True, stop=True)
+            nc.sync.dma_start(base_sb[h][:], base[h * P : (h + 1) * P, :])
 
         big = {}
         small = {}
@@ -175,11 +186,6 @@ def tile_attend_hvblockshares_kernel(tc, taba, dtab, tabb_words, tabb_scales, ta
         for e in range(E):
             nc.tensor.matmul(nwg_t_ps[:], nw[:, e : HALVES * J : E], ident[:], start=(e == 0), stop=(e == E - 1), is_transpose=True)
         for h in range(HALVES):
-            add_turned(h, base_sb[h], True, False)
-        nv = [keep.tile([P, J], F32, name=f"nv{h}", tag=f"targ{HALVES - 1 - h}", align_bytes=64) for h in range(HALVES)]
-        for h in range(HALVES):
-            nc.gpsimd.tensor_tensor(nv[h][:], nw[:, h * J : (h + 1) * J], d[h][:], ALU.mult)
-        for h in range(HALVES):
             nc.scalar.activation(one["m2", h][:], one["xt", h][:], ACT.Copy, scale=piz[:, h : h + 1])
             nc.scalar.activation(one["b1x2", h][:], one["nwt", h][:], ACT.Copy, scale=piz[:, h : h + 1])
             nc.scalar.activation(one["b1", h][:], one["nwt", h][:], ACT.Copy, scale=hpiz[:, h : h + 1])
@@ -187,8 +193,14 @@ def tile_attend_hvblockshares_kernel(tc, taba, dtab, tabb_words, tabb_scales, ta
         nc.scalar.copy(nwg_t[:], nwg_t_ps[:])
         nc.tensor.transpose(nwg_ps[:], nwg_t[:], ident[:])
         for h in range(HALVES):
+            add_turned(h, base_sb[h], True, False)
+        for h in range(HALVES):
             v.tensor_reduce(small["xg", h][:], grouped(big["x", h][:]), AX.X, ALU.add)
+        for h in range(HALVES):
             v.tensor_tensor(small["hm", h][:], small["xg", h][:], rs[:, h, :], ALU.mult)
+        nv = [keep.tile([P, J], F32, name=f"nv{h}", tag=("targ1", "xg1")[h], align_bytes=64) for h in range(HALVES)]
+        for h in range(HALVES):
+            nc.gpsimd.tensor_tensor(nv[h][:], nw[:, h * J : (h + 1) * J], d[h][:], ALU.mult)
 
         def tau(h):
             v.scalar_tensor_tensor(grouped(big["tau", h][:]), grouped(t_ps[h][:]), one["m2", h][:], spread(small["hm", h][:]), ALU.subtract, ALU.subtract)
@@ -204,13 +216,12 @@ def tile_attend_hvblockshares_kernel(tc, taba, dtab, tabb_words, tabb_scales, ta
             return turn_back(h)
 
         tau(0)
-        dw(0)
         tau(1)
+        dw(0)
         a2 = keep.tile([P, HALVES, G], F32, name="a2", tag="m21", align_bytes=64)
         v.tensor_tensor(a2[:], nwg_ps[:].rearrange("p (h g) -> p h g", h=HALVES), rs[:], ALU.mult)
-        back = [ax(0)]
         dw(1)
-        back.append(ax(1))
+        back = [ax(h) for h in range(HALVES)]
         for h in range(HALVES):
             v.tensor_reduce(small["dwg", h][:], grouped(big["dw", h][:]), AX.X, ALU.add)
             v.scalar_tensor_tensor(small["e1", h][:], a2[:, h, :], one["b1", h][:], small["hm", h][:], ALU.add, ALU.mult)

@@ -123,7 +123,7 @@ def tile_attend_hvblockshares_kernel(tc, taba, dtab, tabb_words, tabb_scales, ta
         n_piece(0)
         nc.vector.reciprocal(iz[:], z[:])
         n_piece(1)
-        d_woven = [keep.tile([P, P, PACK], BF16, name=f"d_woven{h}", tag=("z", "root")[h], align_bytes=64) for h in range(HALVES)]
+        d_woven = [keep.tile([P, P, PACK], BF16, name=f"d_woven{h}", tag=("z", "s1g")[h], align_bytes=64) for h in range(HALVES)]
         d_codes = [sb(f"d_codes{h}", [P, P], U32) for h in range(HALVES)]
         d_scales = [sb(f"d_scales{h}", [P, P], U8) for h in range(HALVES)]
         for h in range(HALVES):
@@ -146,7 +146,7 @@ def tile_attend_hvblockshares_kernel(tc, taba, dtab, tabb_words, tabb_scales, ta
                 nc.scalar.activation(d[h][:, cols], dh[h][:, cols], ACT.Square)
         nc.scalar.activation(piz[:], iz[:], ACT.Copy, scale=1.0 / 512.0)
         nc.scalar.activation(hpiz[:], iz[:], ACT.Copy, scale=1.0 / 1024.0)
-        base_sb = [keep.tile([P, J], F32, name=f"base{h}", tag=("d_codes1", "d_scales1")[h], align_bytes=64) for h in range(HALVES)]
+        base_sb = [keep.tile([P, J], F32, name=f"base{h}", tag=("d_plane3", "a_woven1")[h], align_bytes=64) for h in range(HALVES)]
         for h in range(HALVES):
             nc.sync.dma_start(base_sb[h][:], base[h * P : (h + 1) * P, :])
 
@@ -156,15 +156,24 @@ def tile_attend_hvblockshares_kernel(tc, taba, dtab, tabb_words, tabb_scales, ta
         for h in range(HALVES):
             for name in ("x", "tau", "dw", "ax", "dn", "y", "sum_t"):
                 big[name, h] = sb(f"{name}{h}", [P, J])
-            for name in ("xg", "hm", "e1", "dwg", "d1", "dd"):
+            for name in ("xg", "dwg", "d1", "dd"):
                 small[name, h] = sb(f"{name}{h}", [P, G])
             for name in ("xt", "m2", "nwt", "b1", "b1x2", "nb", "dwt", "c2"):
                 one[name, h] = sb(f"{name}{h}", [P, 1])
         nw = sb("nw", [P, HALVES * J])
         acc = [psum.tile([P, J], F32, name=f"acc{h}", tag=f"bank{h}1") for h in range(HALVES)]
-        nwg_t_ps = psum.tile([P, P], F32, name="nwg_t_ps")
-        nwg_ps = psum.tile([P, P], F32, name="nwg_ps")
+        rs_t_ps = psum.tile([P, P], F32, name="rs_t_ps", tag="turned")
+        group_ps = psum.tile([P, 2, HALVES, G], F32, name="group_ps")
+        rs_ps = group_ps[:, 0]
+        nwg_ps = group_ps[:, 1]
+        rs_t = sb("rs_t", [P, P])
+        nc.tensor.transpose(rs_t_ps[:], rs[:].rearrange("p h g -> p (h g)"), ident[:])
+        nc.scalar.copy(rs_t[:], rs_t_ps[:])
+        nc.tensor.transpose(rs_ps.rearrange("p h g -> p (h g)"), rs_t[:], ident[:])
+        nwg_t_ps = psum.tile([P, P], F32, name="nwg_t_ps", tag="turned")
         nwg_t = sb("nwg_t", [P, P])
+        hm = sb("hm", [P, HALVES, G])
+        a1 = sb("a1", [P, HALVES, G])
 
         def add_turned(h, src, first, last):
             for b in range(J // P):
@@ -172,17 +181,19 @@ def tile_attend_hvblockshares_kernel(tc, taba, dtab, tabb_words, tabb_scales, ta
                 nc.tensor.matmul(acc[h][:, cols], src[:, cols], ident[:], start=(first and b == 0), stop=(last and b == J // P - 1), is_transpose=True)
 
         def turn_back(h):
-            nc.scalar.copy(big["sum_t", h][:], acc[h][:])
-            back = psum.tile([P, J], F32, name=f"back{h}", tag=f"bank{h}0")
+            back = [psum.tile([P, J // 2], F32, name=f"back{h}{k}", tag=(f"bank{h}0", f"t_ps{h}")[k]) for k in range(2)]
             for b in range(J // P):
                 cols = slice(b * P, (b + 1) * P)
-                nc.tensor.transpose(back[:, cols], big["sum_t", h][:, cols], ident[:])
+                nc.scalar.copy(big["sum_t", h][:, cols], acc[h][:, cols])
+                nc.tensor.transpose(back[b // 2][:, (b % 2) * P : (b % 2 + 1) * P], big["sum_t", h][:, cols], ident[:])
             return back
 
         v = nc.vector
         for h in range(HALVES):
             v.scalar_tensor_tensor(nw[:, h * J : (h + 1) * J], d[h][:], 1.0, targ_sb[h][:], ALU.subtract, ALU.mult, accum_out=one["nwt", h][:])
             v.scalar_tensor_tensor(big["x", h][:], t_ps[h][:], 0.5, n[h][:], ALU.mult, ALU.mult, accum_out=one["xt", h][:])
+        for h in range(HALVES):
+            add_turned(h, base_sb[h], True, False)
         for e in range(E):
             nc.tensor.matmul(nwg_t_ps[:], nw[:, e : HALVES * J : E], ident[:], start=(e == 0), stop=(e == E - 1), is_transpose=True)
         for h in range(HALVES):
@@ -191,19 +202,17 @@ def tile_attend_hvblockshares_kernel(tc, taba, dtab, tabb_words, tabb_scales, ta
             nc.scalar.activation(one["b1", h][:], one["nwt", h][:], ACT.Copy, scale=hpiz[:, h : h + 1])
             nc.scalar.activation(one["nb", h][:], one["b1", h][:], ACT.Copy, scale=one["m2", h][:])
         nc.scalar.copy(nwg_t[:], nwg_t_ps[:])
-        nc.tensor.transpose(nwg_ps[:], nwg_t[:], ident[:])
-        for h in range(HALVES):
-            add_turned(h, base_sb[h], True, False)
         for h in range(HALVES):
             v.tensor_reduce(small["xg", h][:], grouped(big["x", h][:]), AX.X, ALU.add)
         for h in range(HALVES):
-            v.tensor_tensor(small["hm", h][:], small["xg", h][:], rs[:, h, :], ALU.mult)
-        nv = [keep.tile([P, J], F32, name=f"nv{h}", tag=("targ1", "xg1")[h], align_bytes=64) for h in range(HALVES)]
+            v.tensor_tensor(hm[:, h, :], small["xg", h][:], rs_ps[:, h, :], ALU.mult)
+        nc.tensor.transpose(nwg_ps.rearrange("p h g -> p (h g)"), nwg_t[:], ident[:])
+        nv = [keep.tile([P, J], F32, name=f"nv{h}", tag=("targ1", "targ0")[h], align_bytes=64) for h in range(HALVES)]
         for h in range(HALVES):
             nc.gpsimd.tensor_tensor(nv[h][:], nw[:, h * J : (h + 1) * J], d[h][:], ALU.mult)
 
         def tau(h):
-            v.scalar_tensor_tensor(grouped(big["tau", h][:]), grouped(t_ps[h][:]), one["m2", h][:], spread(small["hm", h][:]), ALU.subtract, ALU.subtract)
+            v.scalar_tensor_tensor(grouped(big["tau", h][:]), grouped(t_ps[h][:]), one["m2", h][:], spread(hm[:, h, :]), ALU.subtract, ALU.subtract)
 
         def dw(h):
             v.scalar_tensor_tensor(big["dw", h][:], nv[h][:], -1.0, big["tau", h][:], ALU.mult, ALU.mult, accum_out=one["dwt", h][:])
@@ -219,21 +228,28 @@ def tile_attend_hvblockshares_kernel(tc, taba, dtab, tabb_words, tabb_scales, ta
         tau(1)
         dw(0)
         a2 = keep.tile([P, HALVES, G], F32, name="a2", tag="m21", align_bytes=64)
-        v.tensor_tensor(a2[:], nwg_ps[:].rearrange("p (h g) -> p h g", h=HALVES), rs[:], ALU.mult)
+        v.tensor_tensor(a2[:], nwg_ps, rs[:], ALU.mult)
+        for h in range(HALVES):
+            nc.scalar.activation(a1[:, h, :], a2[:, h, :], ACT.Identity, bias=one["b1", h][:])
         dw(1)
         back = [ax(h) for h in range(HALVES)]
+        e1 = keep.tile([P, HALVES, G], F32, name="e1", tag="x1", align_bytes=64)
+        nc.gpsimd.tensor_tensor(e1[:], a1[:], hm[:], ALU.mult)
         for h in range(HALVES):
             v.tensor_reduce(small["dwg", h][:], grouped(big["dw", h][:]), AX.X, ALU.add)
-            v.scalar_tensor_tensor(small["e1", h][:], a2[:, h, :], one["b1", h][:], small["hm", h][:], ALU.add, ALU.mult)
         for h in range(HALVES):
-            v.scalar_tensor_tensor(small["d1", h][:], small["dwg", h][:], -0.5, rs[:, h, :], ALU.mult, ALU.mult)
+            v.scalar_tensor_tensor(small["d1", h][:], small["dwg", h][:], -0.5, rs_ps[:, h, :], ALU.mult, ALU.mult)
         for h in range(HALVES):
-            v.tensor_tensor(small["dd", h][:], small["d1", h][:], small["e1", h][:], ALU.subtract)
+            v.tensor_tensor(small["dd", h][:], small["d1", h][:], e1[:, h, :], ALU.subtract)
         for h in range(HALVES):
             v.scalar_tensor_tensor(grouped(big["dn", h][:]), spread(small["dd", h][:]), one["c2", h][:], grouped(n[h][:]), ALU.subtract, ALU.mult)
+        back_sb = sb("back_sb", [P, J // 2])
+        nc.scalar.copy(back_sb[:], back[0][1][:])
         for h in range(HALVES):
-            pieces = 1 + h
-            for k in range(pieces):
-                cols = slice(k * J // pieces, (k + 1) * J // pieces)
-                v.tensor_tensor(big["y", h][:, cols], back[h][:, cols], big["dn", h][:, cols], ALU.add)
+            for k in range(2):
+                cols = slice(k * J // 2, (k + 1) * J // 2)
+                if (h, k) == (0, 1):
+                    nc.gpsimd.tensor_tensor(big["y", h][:, cols], back_sb[:], big["dn", h][:, cols], ALU.add)
+                else:
+                    v.tensor_tensor(big["y", h][:, cols], back[h][k][:], big["dn", h][:, cols], ALU.add)
                 nc.sync.dma_start(out[h * P : (h + 1) * P, cols], big["y", h][:, cols])

@@ -243,13 +243,8 @@ def tile_attend_hvblockshares_kernel(tc, taba, dtab, tabb_words, tabb_scales, ta
             v.tensor_tensor(small["dd", h][:], small["d1", h][:], e1[:, h, :], ALU.subtract)
         for h in range(HALVES):
             v.scalar_tensor_tensor(grouped(big["dn", h][:]), spread(small["dd", h][:]), one["c2", h][:], grouped(n[h][:]), ALU.subtract, ALU.mult)
-        back_sb = sb("back_sb", [P, J // 2])
-        nc.scalar.copy(back_sb[:], back[0][1][:])
         for h in range(HALVES):
             for k in range(2):
                 cols = slice(k * J // 2, (k + 1) * J // 2)
-                if (h, k) == (0, 1):
-                    nc.gpsimd.tensor_tensor(big["y", h][:, cols], back_sb[:], big["dn", h][:, cols], ALU.add)
-                else:
-                    v.tensor_tensor(big["y", h][:, cols], back[h][k][:], big["dn", h][:, cols], ALU.add)
+                v.tensor_tensor(big["y", h][:, cols], back[h][k][:], big["dn", h][:, cols], ALU.add)
                 nc.sync.dma_start(out[h * P : (h + 1) * P, cols], big["y", h][:, cols])

from contextlib import ExitStack

import concourse.mybir as mybir
from concourse.masks import make_identity

D, T, U, I, J, G = 512, 1024, 1024, 256, 512, 64
E = J // G
P = 128
PACK = 4
HALVES = I // P
FLOPS = 2 * 2 * D * I * J

F32 = mybir.dt.float32
BF16 = mybir.dt.bfloat16
I32 = mybir.dt.int32
U32 = mybir.dt.uint32
U16 = mybir.dt.uint16
U8 = mybir.dt.uint8
FP8X4 = mybir.dt.float8_e4m3fn_x4
FP4X4 = mybir.dt.float4_e2m1fn_x4
ACT = mybir.ActivationFunctionType
ALU = mybir.AluOpType
AX = mybir.AxisListType


def tile_attend_hvblockshares_kernel(tc, taba, dtab, tabb_words, tabb_scales, targ, base, offs, offs2, out):
    nc = tc.nc
    with ExitStack() as ctx:
        lists = ctx.enter_context(tc.tile_pool(name="lists", bufs=1))
        keep = ctx.enter_context(tc.tile_pool(name="keep", bufs=1))
        psum = ctx.enter_context(tc.psum_pool(name="psum", bufs=1))

        def sb(name, shape, dtype=F32):
            return keep.tile(shape, dtype, name=name, align_bytes=64)

        def grouped(ap):
            return ap.rearrange("p (g e) -> p g e", e=E)

        def spread(ap):
            return ap.unsqueeze(2).to_broadcast([P, G, E])

        rows_list = lists.tile([P, I // 16], U16, name="rows_list")
        cols_list = lists.tile([P, J // 16], U16, name="cols_list")
        words = sb("words", [P, U], U16)
        scales = sb("scales", [P, U], U8)
        a_planes = [sb(f"a_plane{t}", [P, T]) for t in range(PACK)]
        d_planes = [sb(f"d_plane{t}", [P, T]) for t in range(PACK)]
        targ_sb = [sb(f"targ{h}", [P, J]) for h in range(HALVES)]

        nc.gpsimd.memset(scales[:].bitcast(I32), 0)
        ident = sb("ident", [P, P])
        make_identity(nc, ident[:])
        a_rows = taba.rearrange("(p t) n -> p t n", t=PACK)
        d_rows = dtab.rearrange("(p t) n -> p t n", t=PACK)
        nc.sync.dma_start(cols_list[:], offs2)
        nc.sync.dma_start(words[:].bitcast(I32), tabb_words[0].bitcast(I32))
        nc.sync.dma_start(rows_list[:], offs)
        for t in range(2):
            nc.sync.dma_start(a_planes[t][:], a_rows[:, t, :])
        for q in range(4):
            nc.sync.dma_start(scales[32 * q : 32 * q + 4, :].bitcast(I32), tabb_scales[0, 4 * q : 4 * q + 4, :].bitcast(I32))
        for t in range(2, PACK):
            nc.sync.dma_start(a_planes[t][:], a_rows[:, t, :])
        for t in range(PACK):
            nc.sync.dma_start(d_planes[t][:], d_rows[:, t, :])
        for h in range(HALVES):
            nc.sync.dma_start(targ_sb[h][:], targ[h * P : (h + 1) * P, :])

        b_words = sb("b_words", [P, J], U16)
        b_scales = sb("b_scales", [P, J], U8)
        nc.vector.tensor_copy(b_words[:], words[:].indirect(cols_list[:]))
        nc.vector.tensor_copy(b_scales[:], scales[:].indirect(cols_list[:]))

        a_picked = sb("a_picked", [P, 2, I], BF16)
        a_woven = [sb(f"a_woven{h}", [P, P, PACK], BF16) for h in range(HALVES)]
        for t in range(2):
            nc.scalar.activation(a_picked[:, t, :], a_planes[t][:].indirect(rows_list[:]), ACT.Copy)
        for h in range(HALVES):
            nc.scalar.copy(a_woven[h][:, :, 0:2], a_picked[:, :, h * P : (h + 1) * P].rearrange("p t n -> p n t"))
        for t in range(2, PACK):
            for h in range(HALVES):
                nc.vector.tensor_copy(a_woven[h][:, :, t], a_planes[t][:].indirect(rows_list[:, 8 * h : 8 * h + 8]))
        t_ps = [psum.tile([P, J], F32, name=f"t_ps{h}") for h in range(HALVES)]
        p = [sb(f"p{h}", [P, J]) for h in range(HALVES)]
        s1g = sb("s1g", [P, HALVES, G])
        for h in range(HALVES):
            codes = sb(f"a_codes{h}", [P, P], U32)
            plane = sb(f"a_scales{h}", [P, P], U8)
            nc.vector.quantize_mx(out=codes[:].bitcast(FP8X4), scales=plane[:], in_=a_woven[h][:].rearrange("p n t -> p (n t)"))
            for k in range(2):
                cols = slice(k * J // 2, (k + 1) * J // 2)
                s_ps = psum.tile([P, J // 2], F32, name=f"s_ps{h}{k}", tag=f"bank{h}{k}")
                nc.tensor.matmul_mx(out=s_ps[:], lhsT=codes[:].bitcast(FP8X4), lhsT_scale=plane[:],
                                    rhs=b_words[:, cols].bitcast(FP4X4), rhs_scale=b_scales[:, cols], start=True, stop=True)
                nc.scalar.activation(p[h][:, cols], s_ps[:], ACT.Exp)
        for h in range(HALVES):
            nc.vector.tensor_reduce(s1g[:, h, :], grouped(p[h][:]), AX.X, ALU.add)

        rs = sb("rs", [P, HALVES, G])
        nc.scalar.activation(rs[:], s1g[:], ACT.Abs_reciprocal_sqrt)

        d_picked = keep.tile([P, PACK, I], BF16, name="d_picked", tag="a_woven1", align_bytes=64)
        for t in range(PACK - 1):
            nc.vector.tensor_copy(d_picked[:, t, :], d_planes[t][:].indirect(rows_list[:]))
        nc.scalar.activation(d_picked[:, PACK - 1, :], d_planes[PACK - 1][:].indirect(rows_list[:]), ACT.Copy)

        root = sb("root", [P, HALVES, G])
        z = sb("z", [P, HALVES])
        iz = sb("iz", [P, HALVES])
        piz = sb("piz", [P, HALVES])
        hpiz = sb("hpiz", [P, HALVES])
        n = [sb(f"n{h}", [P, J]) for h in range(HALVES)]
        dh = [sb(f"dh{h}", [P, J]) for h in range(HALVES)]
        d = [sb(f"d{h}", [P, J]) for h in range(HALVES)]
        for h in range(HALVES):
            nc.vector.scalar_tensor_tensor(root[:, h, :], s1g[:, h, :], 1.0 / 512.0, rs[:, h, :], ALU.mult, ALU.mult, accum_out=z[:, h : h + 1])
        def half_of(ap, k):
            return ap[:, k * J // 2 : (k + 1) * J // 2].rearrange("p (g e) -> p g e", e=E)

        def n_piece(k):
            nc.vector.tensor_tensor(half_of(n[0], k), half_of(p[0], k), rs[:, 0, k * G // 2 : (k + 1) * G // 2].unsqueeze(2).to_broadcast([P, G // 2, E]), ALU.mult)

        n_piece(0)
        nc.vector.reciprocal(iz[:], z[:])
        n_piece(1)
        d_woven = [keep.tile([P, P, PACK], BF16, name=f"d_woven{h}", tag=("z", "s1g")[h], align_bytes=64) for h in range(HALVES)]
        d_codes = [sb(f"d_codes{h}", [P, P], U32) for h in range(HALVES)]
        d_scales = [sb(f"d_scales{h}", [P, P], U8) for h in range(HALVES)]
        for h in range(HALVES):
            nc.vector.tensor_copy(d_woven[h][:], d_picked[:, :, h * P : (h + 1) * P].rearrange("p t n -> p n t"))

        def tangent_scores(h):
            nc.vector.quantize_mx(out=d_codes[h][:].bitcast(FP8X4), scales=d_scales[h][:], in_=d_woven[h][:].rearrange("p n t -> p (n t)"))
            nc.tensor.matmul_mx(out=t_ps[h][:], lhsT=d_codes[h][:].bitcast(FP8X4), lhsT_scale=d_scales[h][:],
                                rhs=b_words[:].bitcast(FP4X4), rhs_scale=b_scales[:], start=True, stop=True)

        tangent_scores(0)
        nc.vector.tensor_tensor(grouped(n[1][:]), grouped(p[1][:]), spread(rs[:, 1, :]), ALU.mult)
        tangent_scores(1)
        for h in range(HALVES):
            for k in range(2):
                cols = slice(k * J // 2, (k + 1) * J // 2)
                nc.scalar.activation(dh[h][:, cols], n[h][:, cols], ACT.Abs_reciprocal_sqrt, bias=1.0, scale=iz[:, h : h + 1])
            for k in range(2):
                cols = slice(k * J // 2, (k + 1) * J // 2)
                nc.scalar.activation(d[h][:, cols], dh[h][:, cols], ACT.Square)
        nc.scalar.activation(piz[:], iz[:], ACT.Copy, scale=1.0 / 512.0)
        nc.scalar.activation(hpiz[:], iz[:], ACT.Copy, scale=1.0 / 1024.0)
        base_sb = [keep.tile([P, J], F32, name=f"base{h}", tag=("d_plane3", "a_woven1")[h], align_bytes=64) for h in range(HALVES)]
        for h in range(HALVES):
            nc.sync.dma_start(base_sb[h][:], base[h * P : (h + 1) * P, :])

        big = {}
        small = {}
        one = {}
        for h in range(HALVES):
            for name in ("x", "tau", "dw", "ax", "dn", "y", "sum_t"):
                big[name, h] = sb(f"{name}{h}", [P, J])
            for name in ("xg", "dwg", "d1", "dd"):
                small[name, h] = sb(f"{name}{h}", [P, G])
            for name in ("xt", "m2", "nwt", "b1", "b1x2", "nb", "dwt", "c2"):
                one[name, h] = sb(f"{name}{h}", [P, 1])
        nw = sb("nw", [P, HALVES * J])
        acc = [psum.tile([P, J], F32, name=f"acc{h}", tag=f"bank{h}1") for h in range(HALVES)]
        rs_t_ps = psum.tile([P, P], F32, name="rs_t_ps", tag="turned")
        group_ps = psum.tile([P, 2, HALVES, G], F32, name="group_ps")
        rs_ps = group_ps[:, 0]
        nwg_ps = group_ps[:, 1]
        rs_t = sb("rs_t", [P, P])
        nc.tensor.transpose(rs_t_ps[:], rs[:].rearrange("p h g -> p (h g)"), ident[:])
        nc.scalar.copy(rs_t[:], rs_t_ps[:])
        nc.tensor.transpose(rs_ps.rearrange("p h g -> p (h g)"), rs_t[:], ident[:])
        nwg_t_ps = psum.tile([P, P], F32, name="nwg_t_ps", tag="turned")
        nwg_t = sb("nwg_t", [P, P])
        hm = sb("hm", [P, HALVES, G])
        a1 = sb("a1", [P, HALVES, G])

        def add_turned(h, src, first, last):
            for b in range(J // P):
                cols = slice(b * P, (b + 1) * P)
                nc.tensor.matmul(acc[h][:, cols], src[:, cols], ident[:], start=(first and b == 0), stop=(last and b == J // P - 1), is_transpose=True)

        def turn_back(h):
            back = [psum.tile([P, J // 2], F32, name=f"back{h}{k}", tag=(f"bank{h}0", f"t_ps{h}")[k]) for k in range(2)]
            for b in range(J // P):
                cols = slice(b * P, (b + 1) * P)
                nc.scalar.copy(big["sum_t", h][:, cols], acc[h][:, cols])
                nc.tensor.transpose(back[b // 2][:, (b % 2) * P : (b % 2 + 1) * P], big["sum_t", h][:, cols], ident[:])
            return back

        v = nc.vector
        for h in range(HALVES):
            v.scalar_tensor_tensor(nw[:, h * J : (h + 1) * J], d[h][:], 1.0, targ_sb[h][:], ALU.subtract, ALU.mult, accum_out=one["nwt", h][:])
            v.scalar_tensor_tensor(big["x", h][:], t_ps[h][:], 0.5, n[h][:], ALU.mult, ALU.mult, accum_out=one["xt", h][:])
        for h in range(HALVES):
            add_turned(h, base_sb[h], True, False)
        for e in range(E):
            nc.tensor.matmul(nwg_t_ps[:], nw[:, e : HALVES * J : E], ident[:], start=(e == 0), stop=(e == E - 1), is_transpose=True)
        for h in range(HALVES):
            nc.scalar.activation(one["m2", h][:], one["xt", h][:], ACT.Copy, scale=piz[:, h : h + 1])
            nc.scalar.activation(one["b1x2", h][:], one["nwt", h][:], ACT.Copy, scale=piz[:, h : h + 1])
            nc.scalar.activation(one["b1", h][:], one["nwt", h][:], ACT.Copy, scale=hpiz[:, h : h + 1])
            nc.scalar.activation(one["nb", h][:], one["b1", h][:], ACT.Copy, scale=one["m2", h][:])
        nc.scalar.copy(nwg_t[:], nwg_t_ps[:])
        for h in range(HALVES):
            v.tensor_reduce(small["xg", h][:], grouped(big["x", h][:]), AX.X, ALU.add)
        for h in range(HALVES):
            v.tensor_tensor(hm[:, h, :], small["xg", h][:], rs_ps[:, h, :], ALU.mult)
        nc.tensor.transpose(nwg_ps.rearrange("p h g -> p (h g)"), nwg_t[:], ident[:])
        nv = [keep.tile([P, J], F32, name=f"nv{h}", tag=("targ1", "targ0")[h], align_bytes=64) for h in range(HALVES)]
        for h in range(HALVES):
            nc.gpsimd.tensor_tensor(nv[h][:], nw[:, h * J : (h + 1) * J], d[h][:], ALU.mult)

        def tau(h):
            v.scalar_tensor_tensor(grouped(big["tau", h][:]), grouped(t_ps[h][:]), one["m2", h][:], spread(hm[:, h, :]), ALU.subtract, ALU.subtract)

        def dw(h):
            v.scalar_tensor_tensor(big["dw", h][:], nv[h][:], -1.0, big["tau", h][:], ALU.mult, ALU.mult, accum_out=one["dwt", h][:])
            nc.scalar.activation(one["c2", h][:], one["dwt", h][:], ACT.Identity, bias=one["nb", h][:], scale=hpiz[:, h : h + 1])
            add_turned(h, big["dw", h], False, False)

        def ax(h):
            v.scalar_tensor_tensor(grouped(big["ax", h][:]), spread(a2[:, h, :]), one["b1x2", h][:], grouped(big["x", h][:]), ALU.add, ALU.mult)
            add_turned(h, big["ax", h], False, True)
            return turn_back(h)

        tau(0)
        tau(1)
        dw(0)
        a2 = keep.tile([P, HALVES, G], F32, name="a2", tag="m21", align_bytes=64)
        v.tensor_tensor(a2[:], nwg_ps, rs[:], ALU.mult)
        for h in range(HALVES):
            nc.scalar.activation(a1[:, h, :], a2[:, h, :], ACT.Identity, bias=one["b1", h][:])
        dw(1)
        back = [ax(h) for h in range(HALVES)]
        e1 = keep.tile([P, HALVES, G], F32, name="e1", tag="x1", align_bytes=64)
        nc.gpsimd.tensor_tensor(e1[:], a1[:], hm[:], ALU.mult)
        for h in range(HALVES):
            v.tensor_reduce(small["dwg", h][:], grouped(big["dw", h][:]), AX.X, ALU.add)
        for h in range(HALVES):
            v.scalar_tensor_tensor(small["d1", h][:], small["dwg", h][:], -0.5, rs_ps[:, h, :], ALU.mult, ALU.mult)
        for h in range(HALVES):
            v.tensor_tensor(small["dd", h][:], small["d1", h][:], e1[:, h, :], ALU.subtract)
        for h in range(HALVES):
            v.scalar_tensor_tensor(grouped(big["dn", h][:]), spread(small["dd", h][:]), one["c2", h][:], grouped(n[h][:]), ALU.subtract, ALU.mult)
        for h in range(HALVES):
            for k in range(2):
                cols = slice(k * J // 2, (k + 1) * J // 2)
                v.tensor_tensor(big["y", h][:, cols], back[h][k][:], big["dn", h][:, cols], ALU.add)
                nc.sync.dma_start(out[h * P : (h + 1) * P, cols], big["y", h][:, cols])
